import numpy as np
import ml_dtypes


def mxq(x, axis, fmt="e4m3"):
    dtype, down = {"e4m3": (ml_dtypes.float8_e4m3fn, 7), "e5m2": (ml_dtypes.float8_e5m2, 14)}[fmt]
    v = np.moveaxis(np.asarray(x, np.float32).astype(ml_dtypes.bfloat16).astype(np.float64), axis, -1)
    blocks = v.reshape(v.shape[:-1] + (-1, 32))
    amax = np.abs(blocks).max(-1, keepdims=True)
    byte = np.maximum(np.where(amax > 0, np.frexp(amax)[1] - 1 + 127, 0) - down, 1)
    scale = np.exp2(byte - 127.0)
    codes = (blocks / scale).astype(np.float32).astype(dtype).astype(np.float64)
    return np.moveaxis((codes * scale).reshape(v.shape), -1, axis)


WIDE = False


def mx_kscale(k):
    if not WIDE:
        return np.ones(k)
    levels = np.array([30, -30])
    if k % 512:
        return np.exp2(np.random.permutation(np.resize(levels, k // 32))).repeat(32)
    a = np.empty((k // 512, 16))
    for p in range(k // 512):
        a[p, :8] = np.random.permutation(np.resize(levels, 8))
        for g in range(8):
            far = levels[np.abs(levels - a[p, g]) >= 10]
            a[p, g + 8] = far[np.random.randint(len(far))]
    return np.exp2(a.ravel()).repeat(32)


def f64(x):
    return np.asarray(x).astype(np.float64)


def striped(idx):
    return np.tile(np.asarray(idx).reshape(-1, 16).T, (8, 1)).astype(np.uint16)


def unstriped(offs):
    return offs[:16].T.reshape(-1).astype(np.int64)


E2M1 = np.array([0.0, 0.5, 1.0, 1.5, 2.0, 3.0, 4.0, 6.0, -0.0, -0.5, -1.0, -1.5, -2.0, -3.0, -4.0, -6.0])


def pack_weight(w, fmt):
    k, n = w.shape
    w = f64(np.asarray(w, np.float32).astype(ml_dtypes.bfloat16)).reshape(k // 32, 32, n)
    amax = np.abs(w).max(1)
    if fmt == "e4m3":
        byte = np.frexp(amax)[1] - 1 + 127 - 7
    else:
        mant, ex = np.frexp(amax / 6.0)
        byte = np.where(mant > 0.5, ex, ex - 1) + 127
    byte = np.clip(np.where(amax > 0, byte, 1), 1, 254)
    scaled = (w * np.exp2(127.0 - byte)[:, None, :]).reshape(k, n).astype(np.float32)
    by_word = np.ascontiguousarray(scaled.reshape(k // 512, 128, 4, n).transpose(0, 1, 3, 2))
    if fmt == "e4m3":
        words = by_word.astype(ml_dtypes.float8_e4m3fn).view(np.uint8)
    else:
        c = by_word.astype(ml_dtypes.float4_e2m1fn).view(np.uint8) & 0xF
        words = (c[..., 0::2] | (c[..., 1::2] << 4)).reshape(k // 512, 128, 2 * n)
    return np.ascontiguousarray(words), np.ascontiguousarray(byte.astype(np.uint8).reshape(k // 512, 16, n))


def unpack_weight(words, scales, fmt):
    g, _, n = scales.shape
    words = np.ascontiguousarray(words).reshape(g, 128, n, -1)
    if fmt == "e4m3":
        vals = words.view(ml_dtypes.float8_e4m3fn).astype(np.float64)
    else:
        nib = np.empty((g, 128, n, 4), np.uint8)
        nib[..., 0::2] = words & 0xF
        nib[..., 1::2] = words >> 4
        vals = E2M1[nib]
    vals = vals * np.repeat(np.exp2(scales.astype(np.float64) - 127.0), 8, axis=1)[..., None]
    return vals.transpose(0, 1, 3, 2).reshape(g * 512, n)


def sigmoid(v):
    return 1.0 / (1.0 + np.exp(-v))


K, T, J, R, C, O, N, E = 512, 2048, 256, 512, 512, 256, 256, 1024


def setup_inputs():
    n = np.random.standard_normal
    idx = np.random.permutation(T)[:J]
    idx2 = np.random.permutation(T)[:J]
    idx3 = np.random.permutation(C)[:J]
    idx4 = np.random.permutation(C)[:J]
    idx5 = np.random.permutation(C)[:O]
    idx6 = np.random.permutation(E)[:O]
    fk = mx_kscale(K)
    fr = mx_kscale(R)
    xtp = pack_weight(n((K, T)) / fk[:, None], "e2m1")
    wp = pack_weight(n((K, R)) * 1 / np.sqrt(K) * fk[:, None] * fr, "e4m3")
    wbp = pack_weight(n((R, N)) * 1 / np.sqrt(R) / fr[:, None], "e2m1")
    return {
        "xt_words": xtp[0],
        "xt_scales": xtp[1],
        "w_words": wp[0],
        "w_scales": wp[1],
        "wb_words": wbp[0],
        "wb_scales": wbp[1],
        "tz": (n((N, E))).astype(np.float32),
        "so": (np.random.uniform(0.6, 1.6, (N, 1))).astype(np.float32),
        "bo": (np.random.uniform(-1.0, 1.0, (N, 1))).astype(np.float32),
        "offs": striped(idx),
        "offs2": striped(idx2),
        "offs3": striped(idx3),
        "offs4": striped(idx4),
        "offs5": striped(idx5),
        "offs6": striped(idx6),
    }


def reference(xt_words, xt_scales, w_words, w_scales, wb_words, wb_scales, tz, so, bo, offs, offs2, offs3, offs4, offs5, offs6):
    idx = unstriped(offs)
    idx2 = unstriped(offs2)
    idx3 = unstriped(offs3)
    idx4 = unstriped(offs4)
    idx5 = unstriped(offs5)
    idx6 = unstriped(offs6)
    xtu = unpack_weight(xt_words, xt_scales, "e2m1")
    wu = unpack_weight(w_words, w_scales, "e4m3")
    wbu = unpack_weight(wb_words, wb_scales, "e2m1")
    xtidxg = xtu[:, idx]
    a = wu.T @ xtidxg
    xtidx2g = xtu[:, idx2]
    b = wu.T @ xtidx2g
    pw = np.zeros((R, C))
    pw[:, idx3] = a
    pv = np.zeros((R, C))
    pv[:, idx4] = b
    pg = pw + pv
    hid = pg[:, idx5]
    hidq = mxq(hid, 0, "e5m2")
    p = wbu.T @ hidq
    y = p * sigmoid(f64(tz)[:, idx6] * f64(so) + f64(bo))
    return y

@@ -1,0 +1,175 @@
+from contextlib import ExitStack
+
+import concourse.mybir as mybir
+
+K, T, J, R, C, O, N, E = 512, 2048, 256, 512, 512, 256, 256, 1024
+FLOPS = 2 * K * R * J * 2 + 2 * R * N * O
+
+F32 = mybir.dt.float32
+BF16 = mybir.dt.bfloat16
+I32 = mybir.dt.int32
+U32 = mybir.dt.uint32
+U16 = mybir.dt.uint16
+U8 = mybir.dt.uint8
+E4M3X4 = mybir.dt.float8_e4m3fn_x4
+E5M2X4 = mybir.dt.float8_e5m2_x4
+E2M1X4 = mybir.dt.float4_e2m1fn_x4
+ACT = mybir.ActivationFunctionType
+ALU = mybir.AluOpType
+
+P = 128
+PACK = 4
+SPLIT = 96
+
+
+def load_scale_rows(queue, plane, rows, quadrants=range(4)):
+    for q in quadrants:
+        queue.dma_start(out=plane[32 * q : 32 * q + 4, :].bitcast(I32), in_=rows[4 * q : 4 * q + 4, :].bitcast(I32))
+
+
+def tile_list_tied_shared_one_finalgate_kernel(
+    tc, xt_words, xt_scales, w_words, w_scales, wb_words, wb_scales, tz, so, bo,
+    offs, offs2, offs3, offs4, offs5, offs6, out,
+):
+    nc = tc.nc
+    with ExitStack() as ctx:
+        lists = ctx.enter_context(tc.tile_pool(name="lists", bufs=1))
+        keep = ctx.enter_context(tc.tile_pool(name="keep", bufs=1))
+        psum = ctx.enter_context(tc.psum_pool(name="psum", bufs=1))
+
+        l1 = lists.tile([P, J // 16], U16, name="l1")
+        l2 = lists.tile([P, J // 16], U16, name="l2")
+        l3 = lists.tile([P, J // 16], U16, name="l3")
+        l4 = lists.tile([P, J // 16], U16, name="l4")
+        l5 = lists.tile([P, O // 16], U16, name="l5")
+        l6 = lists.tile([P, O // 16], U16, name="l6")
+
+        xt_w = keep.tile([P, T], U16, name="xt_w", tag="big0", align_bytes=64)
+        xt_s = keep.tile([P, T], U8, name="xt_s", tag="xt_s", align_bytes=64)
+        w_raw = keep.tile([P, R], U32, name="w_raw", tag="big1", align_bytes=64)
+        ws_raw = keep.tile([P, R], U8, name="ws_raw", tag="small", align_bytes=64)
+        wb_s = keep.tile([P, N], U8, name="wb_s", align_bytes=64)
+        pw = [keep.tile([P, C], F32, name="pw%d" % t, align_bytes=64) for t in range(3)]
+        pv = [keep.tile([P, C], F32, name="pv%d" % t, align_bytes=64) for t in range(3)]
+        pg = [keep.tile([P, C], F32, name="pg%d" % t, align_bytes=64) for t in range(PACK)]
+
+        nc.vector.memset(ws_raw[:].bitcast(I32), 0)
+        nc.gpsimd.memset(xt_s[:, 0 : T // 2].bitcast(I32), 0)
+        nc.vector.memset(xt_s[:, T // 2 :].bitcast(I32), 0)
+
+        for tile, offsets in ((l1, offs), (l2, offs2), (l3, offs3), (l4, offs4)):
+            nc.sync.dma_start(tile[:], offsets)
+        nc.sync.dma_start(out=xt_w[:].bitcast(I32), in_=xt_words[0].bitcast(I32))
+        for tile, offsets in ((l5, offs5), (l6, offs6)):
+            nc.sync.dma_start(tile[:], offsets)
+        nc.sync.dma_start(out=w_raw[:].bitcast(I32), in_=w_words[0].rearrange("p n t -> p (n t)").bitcast(I32))
+        load_scale_rows(nc.sync, xt_s, xt_scales[0])
+        load_scale_rows(nc.sync, ws_raw, w_scales[0], range(0, 3))
+        load_scale_rows(nc.gpsimd, ws_raw, w_scales[0], range(3, 4))
+        for page_a, page_b in zip(pw, pv):
+            nc.vector.memset(page_a[:], 0.0)
+            nc.gpsimd.memset(page_b[:], 0.0)
+        nc.vector.memset(wb_s[:].bitcast(I32), 0)
+        load_scale_rows(nc.sync, wb_s, wb_scales[0])
+
+        xa_w = keep.tile([P, J], U16, name="xa_w", align_bytes=64)
+        xa_s = keep.tile([P, J], U8, name="xa_s", tag="xa_s", align_bytes=64)
+        xb_w = keep.tile([P, J], U16, name="xb_w", align_bytes=64)
+        xb_s = keep.tile([P, J], U8, name="xb_s", align_bytes=64)
+        w_w = keep.tile([P, R], U32, name="w_w", align_bytes=64)
+        w_s = keep.tile([P, R], U8, name="w_s", align_bytes=64)
+
+        dealt_s = w_s[:].rearrange("p (t u v) -> p u t v", t=PACK, v=16)
+        given_s = ws_raw[:].rearrange("p (u v t) -> p u t v", t=PACK, v=16)
+        nc.vector.tensor_copy(out=dealt_s[:, :, 0, :], in_=given_s[:, :, 0, :])
+        nc.vector.tensor_copy(out=dealt_s[:, :, 1:, :], in_=given_s[:, :, 1:, :])
+        nc.vector.tensor_copy(xa_w[:], xt_w[:].indirect(l1[:]))
+        nc.vector.tensor_copy(xa_s[:], xt_s[:].indirect(l1[:]))
+        nc.scalar.copy(
+            out=w_w[:].rearrange("p (t u v) -> p u t v", t=PACK, v=4),
+            in_=w_raw[:].rearrange("p (u v t) -> p u t v", t=PACK, v=4),
+        )
+        nc.vector.tensor_copy(xb_w[:], xt_w[:].indirect(l2[:]))
+        nc.vector.tensor_copy(xb_s[:], xt_s[:].indirect(l2[:]))
+
+        wb_w = keep.tile([P, 2 * N], U8, name="wb_w", tag="small", align_bytes=64)
+        nc.sync.dma_start(out=wb_w[:].bitcast(I32), in_=wb_words[0].bitcast(I32))
+        tz_sb = [keep.tile([P, E], F32, name="tz%d" % h, tag="big%d" % h, align_bytes=64) for h in range(2)]
+        for h in range(2):
+            nc.sync.dma_start(out=tz_sb[h][:], in_=tz[P * h : P * (h + 1), :])
+
+        def first_product(acc, t, words, scales):
+            cols = slice(P * t, P * (t + 1))
+            nc.tensor.matmul_mx(
+                out=acc, lhsT=w_w[:, cols].bitcast(E4M3X4), lhsT_scale=w_s[:, cols],
+                rhs=words[:].bitcast(E2M1X4), rhs_scale=scales[:], start=True, stop=True,
+            )
+
+        acc = [psum.tile([P, 2, J], F32, name="acc%d" % t, tag="acc%d" % t) for t in range(PACK)]
+        acc_b0 = psum.tile([P, J], F32, name="acc_b0")
+        for t in range(PACK):
+            first_product(acc[t][:, 0, :], t, xa_w, xa_s)
+            first_product(acc_b0[:] if t == 0 else acc[t][:, 1, :], t, xb_w, xb_s)
+
+        so_sb = keep.tile([P, 2], F32, name="so_sb", tag="xt_s", align_bytes=64)
+        bo_sb = keep.tile([P, 2], F32, name="bo_sb", tag="xa_s", align_bytes=64)
+        with nc.allow_non_contiguous_dma(reason="one slope and one offset a partition"):
+            nc.sync.dma_start(out=so_sb[:], in_=so.rearrange("(h p) o -> p (h o)", p=P))
+            nc.sync.dma_start(out=bo_sb[:], in_=bo.rearrange("(h p) o -> p (h o)", p=P))
+
+        woven = keep.tile([P, O, PACK], BF16, name="woven", align_bytes=64)
+        half = O // 2
+
+        for t in range(PACK):
+            page_a, page_b = pw[t % 3], pv[t % 3]
+            if t == 0:
+                a0 = keep.tile([P, J], F32, name="a0", tag="ab1", align_bytes=64)
+                b0 = keep.tile([P, J], F32, name="b0", align_bytes=64)
+                nc.scalar.copy(a0[:], acc[t][:, 0, :])
+                nc.vector.tensor_copy(b0[:], acc_b0[:])
+                a_t, b_t = a0[:], b0[:]
+            else:
+                ab = keep.tile([P, 2, J], F32, name="ab%d" % t, tag="ab%d" % t, align_bytes=64)
+                nc.scalar.copy(ab[:], acc[t][:])
+                a_t, b_t = ab[:, 0, :], ab[:, 1, :]
+            if t < PACK - 1:
+                nc.vector.tensor_copy(page_b[:].indirect(l4[:]), b_t)
+            else:
+                nc.scalar.activation(out=page_b[:].indirect(l4[:, SPLIT // 16 :]), in_=b_t[:, SPLIT:], func=ACT.Copy)
+                nc.vector.tensor_copy(page_b[:].indirect(l4[:, 0 : SPLIT // 16]), b_t[:, 0:SPLIT])
+            nc.scalar.activation(out=page_a[:].indirect(l3[:]), in_=a_t, func=ACT.Copy)
+            nc.vector.tensor_tensor(pg[t][:], page_a[:], page_b[:], ALU.add)
+            if t < PACK - 1:
+                nc.vector.tensor_copy(woven[:, :, t], pg[t][:].indirect(l5[:]))
+            else:
+                for u in range(2):
+                    nc.vector.tensor_copy(woven[:, half * u : half * (u + 1), t], pg[t][:].indirect(l5[:, 8 * u : 8 * (u + 1)]))
+
+        gate = keep.tile([P, 2, O], F32, name="gate", tag="ab3", align_bytes=64)
+        for h in range(2):
+            nc.scalar.activation(
+                out=gate[:, h, :], in_=tz_sb[h][:].indirect(l6[:]), func=ACT.Sigmoid,
+                bias=bo_sb[:, h : h + 1], scale=so_sb[:, h : h + 1],
+            )
+
+        h_w = [keep.tile([P, half], U32, name="h_w%d" % u, align_bytes=64) for u in range(2)]
+        h_s = [keep.tile([P, half], U8, name="h_s%d" % u, align_bytes=64) for u in range(2)]
+        for u in range(2):
+            nc.vector.quantize_mx(
+                out=h_w[u][:].bitcast(E5M2X4), scales=h_s[u][:],
+                in_=woven[:, half * u : half * (u + 1), :].rearrange("p o t -> p (o t)"),
+            )
+        out_rows = out.rearrange("(h p) o -> p h o", p=P)
+        for u in range(2):
+            cols = slice(half * u, half * (u + 1))
+            acc_p = psum.tile([P, 2, half], F32, name="acc_p%d" % u)
+            for h in range(2):
+                nc.tensor.matmul_mx(
+                    out=acc_p[:, h, :], lhsT=wb_w[:, 2 * P * h : 2 * P * (h + 1)].bitcast(E2M1X4),
+                    lhsT_scale=wb_s[:, P * h : P * (h + 1)],
+                    rhs=h_w[u][:].bitcast(E5M2X4), rhs_scale=h_s[u][:], start=True, stop=True,
+                )
+            res = keep.tile([P, 2, half], F32, name="res%d" % u, align_bytes=64)
+            nc.vector.tensor_tensor(res[:], acc_p[:], gate[:, :, cols], ALU.mult)
+            queue = nc.sync if u == 0 else nc.scalar
+            queue.dma_start(out=out_rows[:, :, cols], in_=res[:])

@@ -19,7 +19,6 @@ ALU = mybir.AluOpType
 
 P = 128
 PACK = 4
-SPLIT = 96
 
 
 def load_scale_rows(queue, plane, rows, quadrants=range(4)):
@@ -54,6 +53,10 @@ def tile_list_tied_shared_one_finalgate_kernel(
         pg = [keep.tile([P, C], F32, name="pg%d" % t, align_bytes=64) for t in range(PACK)]
 
         nc.vector.memset(ws_raw[:].bitcast(I32), 0)
+        warm_in = keep.tile([P, 1], F32, name="warm_in")
+        warm_out = keep.tile([P, 1], F32, name="warm_out")
+        nc.gpsimd.memset(warm_in[:], 0.0)
+        nc.scalar.activation(out=warm_out[:], in_=warm_in[:], func=ACT.Sigmoid)
         nc.gpsimd.memset(xt_s[:, 0 : T // 2].bitcast(I32), 0)
         nc.vector.memset(xt_s[:, T // 2 :].bitcast(I32), 0)
 
@@ -105,11 +108,11 @@ def tile_list_tied_shared_one_finalgate_kernel(
                 rhs=words[:].bitcast(E2M1X4), rhs_scale=scales[:], start=True, stop=True,
             )
 
-        acc = [psum.tile([P, 2, J], F32, name="acc%d" % t, tag="acc%d" % t) for t in range(PACK)]
-        acc_b0 = psum.tile([P, J], F32, name="acc_b0")
+        acc_a = [psum.tile([P, J], F32, name="acc_a%d" % t, tag="acc_a%d" % t) for t in range(PACK)]
+        acc_b = [psum.tile([P, J], F32, name="acc_b%d" % t, tag="acc_b%d" % t) for t in range(PACK)]
         for t in range(PACK):
-            first_product(acc[t][:, 0, :], t, xa_w, xa_s)
-            first_product(acc_b0[:] if t == 0 else acc[t][:, 1, :], t, xb_w, xb_s)
+            first_product(acc_a[t][:], t, xa_w, xa_s)
+            first_product(acc_b[t][:], t, xb_w, xb_s)
 
         so_sb = keep.tile([P, 2], F32, name="so_sb", tag="xt_s", align_bytes=64)
         bo_sb = keep.tile([P, 2], F32, name="bo_sb", tag="xa_s", align_bytes=64)
@@ -122,30 +125,24 @@ def tile_list_tied_shared_one_finalgate_kernel(
 
         for t in range(PACK):
             page_a, page_b = pw[t % 3], pv[t % 3]
-            if t == 0:
-                a0 = keep.tile([P, J], F32, name="a0", tag="ab1", align_bytes=64)
-                b0 = keep.tile([P, J], F32, name="b0", align_bytes=64)
-                nc.scalar.copy(a0[:], acc[t][:, 0, :])
-                nc.vector.tensor_copy(b0[:], acc_b0[:])
-                a_t, b_t = a0[:], b0[:]
-            else:
-                ab = keep.tile([P, 2, J], F32, name="ab%d" % t, tag="ab%d" % t, align_bytes=64)
-                nc.scalar.copy(ab[:], acc[t][:])
-                a_t, b_t = ab[:, 0, :], ab[:, 1, :]
+            a_t = keep.tile([P, J], F32, name="a%d" % t, tag="a%d" % max(t, 1), align_bytes=64)
+            b_t = keep.tile([P, J], F32, name="b%d" % t, tag="b%d" % max(t, 1), align_bytes=64)
+            nc.scalar.copy(a_t[:], acc_a[t][:])
+            nc.vector.tensor_copy(b_t[:], acc_b[t][:])
+            nc.scalar.activation(out=page_a[:].indirect(l3[:]), in_=a_t[:], func=ACT.Copy)
             if t < PACK - 1:
-                nc.vector.tensor_copy(page_b[:].indirect(l4[:]), b_t)
+                nc.vector.tensor_copy(page_b[:].indirect(l4[:]), b_t[:])
+                nc.gpsimd.tensor_tensor(pg[t][:], page_a[:], page_b[:], ALU.add)
             else:
-                nc.scalar.activation(out=page_b[:].indirect(l4[:, SPLIT // 16 :]), in_=b_t[:, SPLIT:], func=ACT.Copy)
-                nc.vector.tensor_copy(page_b[:].indirect(l4[:, 0 : SPLIT // 16]), b_t[:, 0:SPLIT])
-            nc.scalar.activation(out=page_a[:].indirect(l3[:]), in_=a_t, func=ACT.Copy)
-            nc.vector.tensor_tensor(pg[t][:], page_a[:], page_b[:], ALU.add)
+                nc.scalar.activation(out=page_b[:].indirect(l4[:]), in_=b_t[:], func=ACT.Copy)
+                nc.vector.tensor_tensor(pg[t][:], page_a[:], page_b[:], ALU.add)
             if t < PACK - 1:
                 nc.vector.tensor_copy(woven[:, :, t], pg[t][:].indirect(l5[:]))
             else:
                 for u in range(2):
                     nc.vector.tensor_copy(woven[:, half * u : half * (u + 1), t], pg[t][:].indirect(l5[:, 8 * u : 8 * (u + 1)]))
 
-        gate = keep.tile([P, 2, O], F32, name="gate", tag="ab3", align_bytes=64)
+        gate = keep.tile([P, 2, O], F32, name="gate", tag="b3", align_bytes=64)
         for h in range(2):
             nc.scalar.activation(
                 out=gate[:, h, :], in_=tz_sb[h][:].indirect(l6[:]), func=ACT.Sigmoid,
@@ -162,7 +159,7 @@ def tile_list_tied_shared_one_finalgate_kernel(
         out_rows = out.rearrange("(h p) o -> p h o", p=P)
         for u in range(2):
             cols = slice(half * u, half * (u + 1))
-            acc_p = psum.tile([P, 2, half], F32, name="acc_p%d" % u)
+            acc_p = psum.tile([P, 2, half], F32, name="acc_p%d" % u, tag="acc_a%d" % u)
             for h in range(2):
                 nc.tensor.matmul_mx(
                     out=acc_p[:, h, :], lhsT=wb_w[:, 2 * P * h : 2 * P * (h + 1)].bitcast(E2M1X4),

@@ -53,10 +53,6 @@ def tile_list_tied_shared_one_finalgate_kernel(
         pg = [keep.tile([P, C], F32, name="pg%d" % t, align_bytes=64) for t in range(PACK)]
 
         nc.vector.memset(ws_raw[:].bitcast(I32), 0)
-        warm_in = keep.tile([P, 1], F32, name="warm_in")
-        warm_out = keep.tile([P, 1], F32, name="warm_out")
-        nc.gpsimd.memset(warm_in[:], 0.0)
-        nc.scalar.activation(out=warm_out[:], in_=warm_in[:], func=ACT.Sigmoid)
         nc.gpsimd.memset(xt_s[:, 0 : T // 2].bitcast(I32), 0)
         nc.vector.memset(xt_s[:, T // 2 :].bitcast(I32), 0)
 

@@ -124,7 +124,10 @@ def tile_list_tied_shared_one_finalgate_kernel(
             a_t = keep.tile([P, J], F32, name="a%d" % t, tag="a%d" % max(t, 1), align_bytes=64)
             b_t = keep.tile([P, J], F32, name="b%d" % t, tag="b%d" % max(t, 1), align_bytes=64)
             nc.scalar.copy(a_t[:], acc_a[t][:])
-            nc.vector.tensor_copy(b_t[:], acc_b[t][:])
+            if t < PACK - 1:
+                nc.vector.tensor_copy(b_t[:], acc_b[t][:])
+            else:
+                nc.scalar.copy(b_t[:], acc_b[t][:])
             nc.scalar.activation(out=page_a[:].indirect(l3[:]), in_=a_t[:], func=ACT.Copy)
             if t < PACK - 1:
                 nc.vector.tensor_copy(page_b[:].indirect(l4[:]), b_t[:])
@@ -155,14 +158,14 @@ def tile_list_tied_shared_one_finalgate_kernel(
         out_rows = out.rearrange("(h p) o -> p h o", p=P)
         for u in range(2):
             cols = slice(half * u, half * (u + 1))
-            acc_p = psum.tile([P, 2, half], F32, name="acc_p%d" % u, tag="acc_a%d" % u)
+            res = keep.tile([P, 2, half], F32, name="res%d" % u, align_bytes=64)
             for h in range(2):
+                acc_p = psum.tile([P, half], F32, name="acc_p%d%d" % (u, h), tag="acc_a%d" % (2 * u + h))
                 nc.tensor.matmul_mx(
-                    out=acc_p[:, h, :], lhsT=wb_w[:, 2 * P * h : 2 * P * (h + 1)].bitcast(E2M1X4),
+                    out=acc_p[:], lhsT=wb_w[:, 2 * P * h : 2 * P * (h + 1)].bitcast(E2M1X4),
                     lhsT_scale=wb_s[:, P * h : P * (h + 1)],
                     rhs=h_w[u][:].bitcast(E5M2X4), rhs_scale=h_s[u][:], start=True, stop=True,
                 )
-            res = keep.tile([P, 2, half], F32, name="res%d" % u, align_bytes=64)
-            nc.vector.tensor_tensor(res[:], acc_p[:], gate[:, :, cols], ALU.mult)
+                nc.vector.tensor_tensor(res[:, h, :], acc_p[:], gate[:, h, cols], ALU.mult)
             queue = nc.sync if u == 0 else nc.scalar
             queue.dma_start(out=out_rows[:, :, cols], in_=res[:])

from contextlib import ExitStack

import concourse.mybir as mybir

K, T, J, R, C, O, N, E = 512, 2048, 256, 512, 512, 256, 256, 1024
FLOPS = 2 * K * R * J * 2 + 2 * R * N * O

F32 = mybir.dt.float32
BF16 = mybir.dt.bfloat16
I32 = mybir.dt.int32
U32 = mybir.dt.uint32
U16 = mybir.dt.uint16
U8 = mybir.dt.uint8
E4M3X4 = mybir.dt.float8_e4m3fn_x4
E5M2X4 = mybir.dt.float8_e5m2_x4
E2M1X4 = mybir.dt.float4_e2m1fn_x4
ACT = mybir.ActivationFunctionType
ALU = mybir.AluOpType

P = 128
PACK = 4


def load_scale_rows(queue, plane, rows, quadrants=range(4)):
    for q in quadrants:
        queue.dma_start(out=plane[32 * q : 32 * q + 4, :].bitcast(I32), in_=rows[4 * q : 4 * q + 4, :].bitcast(I32))


def tile_list_tied_shared_one_finalgate_kernel(
    tc, xt_words, xt_scales, w_words, w_scales, wb_words, wb_scales, tz, so, bo,
    offs, offs2, offs3, offs4, offs5, offs6, out,
):
    nc = tc.nc
    with ExitStack() as ctx:
        lists = ctx.enter_context(tc.tile_pool(name="lists", bufs=1))
        keep = ctx.enter_context(tc.tile_pool(name="keep", bufs=1))
        psum = ctx.enter_context(tc.psum_pool(name="psum", bufs=1))

        l1 = lists.tile([P, J // 16], U16, name="l1")
        l2 = lists.tile([P, J // 16], U16, name="l2")
        l3 = lists.tile([P, J // 16], U16, name="l3")
        l4 = lists.tile([P, J // 16], U16, name="l4")
        l5 = lists.tile([P, O // 16], U16, name="l5")
        l6 = lists.tile([P, O // 16], U16, name="l6")

        xt_w = keep.tile([P, T], U16, name="xt_w", tag="big0", align_bytes=64)
        xt_s = keep.tile([P, T], U8, name="xt_s", tag="xt_s", align_bytes=64)
        w_raw = keep.tile([P, R], U32, name="w_raw", tag="big1", align_bytes=64)
        ws_raw = keep.tile([P, R], U8, name="ws_raw", tag="small", align_bytes=64)
        wb_s = keep.tile([P, N], U8, name="wb_s", align_bytes=64)
        pw = [keep.tile([P, C], F32, name="pw%d" % t, align_bytes=64) for t in range(3)]
        pv = [keep.tile([P, C], F32, name="pv%d" % t, align_bytes=64) for t in range(3)]
        pg = [keep.tile([P, C], F32, name="pg%d" % t, align_bytes=64) for t in range(PACK)]

        nc.vector.memset(ws_raw[:].bitcast(I32), 0)
        nc.gpsimd.memset(xt_s[:, 0 : T // 2].bitcast(I32), 0)
        nc.vector.memset(xt_s[:, T // 2 :].bitcast(I32), 0)

        for tile, offsets in ((l1, offs), (l2, offs2), (l3, offs3), (l4, offs4)):
            nc.sync.dma_start(tile[:], offsets)
        nc.sync.dma_start(out=xt_w[:].bitcast(I32), in_=xt_words[0].bitcast(I32))
        for tile, offsets in ((l5, offs5), (l6, offs6)):
            nc.sync.dma_start(tile[:], offsets)
        nc.sync.dma_start(out=w_raw[:].bitcast(I32), in_=w_words[0].rearrange("p n t -> p (n t)").bitcast(I32))
        load_scale_rows(nc.sync, xt_s, xt_scales[0])
        load_scale_rows(nc.sync, ws_raw, w_scales[0], range(0, 3))
        load_scale_rows(nc.gpsimd, ws_raw, w_scales[0], range(3, 4))
        for page_a, page_b in zip(pw, pv):
            nc.vector.memset(page_a[:], 0.0)
            nc.gpsimd.memset(page_b[:], 0.0)
        nc.vector.memset(wb_s[:].bitcast(I32), 0)
        load_scale_rows(nc.sync, wb_s, wb_scales[0])

        xa_w = keep.tile([P, J], U16, name="xa_w", align_bytes=64)
        xa_s = keep.tile([P, J], U8, name="xa_s", tag="xa_s", align_bytes=64)
        xb_w = keep.tile([P, J], U16, name="xb_w", align_bytes=64)
        xb_s = keep.tile([P, J], U8, name="xb_s", align_bytes=64)
        w_w = keep.tile([P, R], U32, name="w_w", align_bytes=64)
        w_s = keep.tile([P, R], U8, name="w_s", align_bytes=64)

        dealt_s = w_s[:].rearrange("p (t u v) -> p u t v", t=PACK, v=16)
        given_s = ws_raw[:].rearrange("p (u v t) -> p u t v", t=PACK, v=16)
        nc.vector.tensor_copy(out=dealt_s[:, :, 0, :], in_=given_s[:, :, 0, :])
        nc.vector.tensor_copy(out=dealt_s[:, :, 1:, :], in_=given_s[:, :, 1:, :])
        nc.vector.tensor_copy(xa_w[:], xt_w[:].indirect(l1[:]))
        nc.vector.tensor_copy(xa_s[:], xt_s[:].indirect(l1[:]))
        nc.scalar.copy(
            out=w_w[:].rearrange("p (t u v) -> p u t v", t=PACK, v=4),
            in_=w_raw[:].rearrange("p (u v t) -> p u t v", t=PACK, v=4),
        )
        nc.vector.tensor_copy(xb_w[:], xt_w[:].indirect(l2[:]))
        nc.vector.tensor_copy(xb_s[:], xt_s[:].indirect(l2[:]))

        wb_w = keep.tile([P, 2 * N], U8, name="wb_w", tag="small", align_bytes=64)
        nc.sync.dma_start(out=wb_w[:].bitcast(I32), in_=wb_words[0].bitcast(I32))
        tz_sb = [keep.tile([P, E], F32, name="tz%d" % h, tag="big%d" % h, align_bytes=64) for h in range(2)]
        for h in range(2):
            nc.sync.dma_start(out=tz_sb[h][:], in_=tz[P * h : P * (h + 1), :])

        def first_product(acc, t, words, scales):
            cols = slice(P * t, P * (t + 1))
            nc.tensor.matmul_mx(
                out=acc, lhsT=w_w[:, cols].bitcast(E4M3X4), lhsT_scale=w_s[:, cols],
                rhs=words[:].bitcast(E2M1X4), rhs_scale=scales[:], start=True, stop=True,
            )

        acc_a = [psum.tile([P, J], F32, name="acc_a%d" % t, tag="acc_a%d" % t) for t in range(PACK)]
        acc_b = [psum.tile([P, J], F32, name="acc_b%d" % t, tag="acc_b%d" % t) for t in range(PACK)]
        for t in range(PACK):
            first_product(acc_a[t][:], t, xa_w, xa_s)
            first_product(acc_b[t][:], t, xb_w, xb_s)

        so_sb = keep.tile([P, 2], F32, name="so_sb", tag="xt_s", align_bytes=64)
        bo_sb = keep.tile([P, 2], F32, name="bo_sb", tag="xa_s", align_bytes=64)
        with nc.allow_non_contiguous_dma(reason="one slope and one offset a partition"):
            nc.sync.dma_start(out=so_sb[:], in_=so.rearrange("(h p) o -> p (h o)", p=P))
            nc.sync.dma_start(out=bo_sb[:], in_=bo.rearrange("(h p) o -> p (h o)", p=P))

        woven = keep.tile([P, O, PACK], BF16, name="woven", align_bytes=64)
        half = O // 2

        for t in range(PACK):
            page_a, page_b = pw[t % 3], pv[t % 3]
            a_t = keep.tile([P, J], F32, name="a%d" % t, tag="a%d" % max(t, 1), align_bytes=64)
            b_t = keep.tile([P, J], F32, name="b%d" % t, tag="b%d" % max(t, 1), align_bytes=64)
            nc.scalar.copy(a_t[:], acc_a[t][:])
            if t < PACK - 1:
                nc.vector.tensor_copy(b_t[:], acc_b[t][:])
            else:
                nc.scalar.copy(b_t[:], acc_b[t][:])
            nc.scalar.activation(out=page_a[:].indirect(l3[:]), in_=a_t[:], func=ACT.Copy)
            if t < PACK - 1:
                nc.vector.tensor_copy(page_b[:].indirect(l4[:]), b_t[:])
                nc.gpsimd.tensor_tensor(pg[t][:], page_a[:], page_b[:], ALU.add)
            else:
                nc.scalar.activation(out=page_b[:].indirect(l4[:]), in_=b_t[:], func=ACT.Copy)
                nc.vector.tensor_tensor(pg[t][:], page_a[:], page_b[:], ALU.add)
            if t < PACK - 1:
                nc.vector.tensor_copy(woven[:, :, t], pg[t][:].indirect(l5[:]))
            else:
                for u in range(2):
                    nc.vector.tensor_copy(woven[:, half * u : half * (u + 1), t], pg[t][:].indirect(l5[:, 8 * u : 8 * (u + 1)]))

        gate = keep.tile([P, 2, O], F32, name="gate", tag="b3", align_bytes=64)
        for h in range(2):
            nc.scalar.activation(
                out=gate[:, h, :], in_=tz_sb[h][:].indirect(l6[:]), func=ACT.Sigmoid,
                bias=bo_sb[:, h : h + 1], scale=so_sb[:, h : h + 1],
            )

        h_w = [keep.tile([P, half], U32, name="h_w%d" % u, align_bytes=64) for u in range(2)]
        h_s = [keep.tile([P, half], U8, name="h_s%d" % u, align_bytes=64) for u in range(2)]
        for u in range(2):
            nc.vector.quantize_mx(
                out=h_w[u][:].bitcast(E5M2X4), scales=h_s[u][:],
                in_=woven[:, half * u : half * (u + 1), :].rearrange("p o t -> p (o t)"),
            )
        out_rows = out.rearrange("(h p) o -> p h o", p=P)
        for u in range(2):
            cols = slice(half * u, half * (u + 1))
            res = keep.tile([P, 2, half], F32, name="res%d" % u, align_bytes=64)
            for h in range(2):
                acc_p = psum.tile([P, half], F32, name="acc_p%d%d" % (u, h), tag="acc_a%d" % (2 * u + h))
                nc.tensor.matmul_mx(
                    out=acc_p[:], lhsT=wb_w[:, 2 * P * h : 2 * P * (h + 1)].bitcast(E2M1X4),
                    lhsT_scale=wb_s[:, P * h : P * (h + 1)],
                    rhs=h_w[u][:].bitcast(E5M2X4), rhs_scale=h_s[u][:], start=True, stop=True,
                )
                nc.vector.tensor_tensor(res[:, h, :], acc_p[:], gate[:, h, cols], ALU.mult)
            queue = nc.sync if u == 0 else nc.scalar
            queue.dma_start(out=out_rows[:, :, cols], in_=res[:])
